import numpy as np
import ml_dtypes


def mxq(x, axis, fmt="e4m3"):
    dtype, down = {"e4m3": (ml_dtypes.float8_e4m3fn, 7), "e5m2": (ml_dtypes.float8_e5m2, 14)}[fmt]
    v = np.moveaxis(np.asarray(x, np.float32).astype(ml_dtypes.bfloat16).astype(np.float64), axis, -1)
    blocks = v.reshape(v.shape[:-1] + (-1, 32))
    amax = np.abs(blocks).max(-1, keepdims=True)
    byte = np.maximum(np.where(amax > 0, np.frexp(amax)[1] - 1 + 127, 0) - down, 1)
    scale = np.exp2(byte - 127.0)
    codes = (blocks / scale).astype(np.float32).astype(dtype).astype(np.float64)
    return np.moveaxis((codes * scale).reshape(v.shape), -1, axis)


WIDE = False


def mx_kscale(k):
    if not WIDE:
        return np.ones(k)
    levels = np.array([10, -10, 5, -5, 0])
    if k % 512:
        return np.exp2(np.random.permutation(np.resize(levels, k // 32))).repeat(32)
    a = np.empty((k // 512, 16))
    for p in range(k // 512):
        a[p, :8] = np.random.permutation(np.resize(levels, 8))
        for g in range(8):
            far = levels[np.abs(levels - a[p, g]) >= 10]
            a[p, g + 8] = far[np.random.randint(len(far))]
    return np.exp2(a.ravel()).repeat(32)


BF16 = ml_dtypes.bfloat16


def bf(x):
    return np.asarray(x, np.float32).astype(BF16)


def f64(x):
    return np.asarray(x).astype(np.float64)


E2M1 = np.array([0.0, 0.5, 1.0, 1.5, 2.0, 3.0, 4.0, 6.0, -0.0, -0.5, -1.0, -1.5, -2.0, -3.0, -4.0, -6.0])


def pack_weight(w, fmt):
    k, n = w.shape
    w = f64(bf(w)).reshape(k // 32, 32, n)
    amax = np.abs(w).max(1)
    if fmt == "e4m3":
        byte = np.frexp(amax)[1] - 1 + 127 - 7
    else:
        mant, ex = np.frexp(amax / 6.0)
        byte = np.where(mant > 0.5, ex, ex - 1) + 127
    byte = np.clip(np.where(amax > 0, byte, 1), 1, 254)
    scaled = (w * np.exp2(127.0 - byte)[:, None, :]).reshape(k, n).astype(np.float32)
    by_word = np.ascontiguousarray(scaled.reshape(k // 512, 128, 4, n).transpose(0, 1, 3, 2))
    if fmt == "e4m3":
        words = by_word.astype(ml_dtypes.float8_e4m3fn).view(np.uint8)
    else:
        c = by_word.astype(ml_dtypes.float4_e2m1fn).view(np.uint8) & 0xF
        words = c[..., 0::2] | (c[..., 1::2] << 4)
    return np.ascontiguousarray(words), np.ascontiguousarray(byte.astype(np.uint8).reshape(k // 512, 16, n))


def unpack_weight(words, scales, fmt):
    g, p, n, _ = words.shape
    if fmt == "e4m3":
        vals = np.ascontiguousarray(words).view(ml_dtypes.float8_e4m3fn).astype(np.float64)
    else:
        nib = np.empty((g, p, n, 4), np.uint8)
        nib[..., 0::2] = words & 0xF
        nib[..., 1::2] = words >> 4
        vals = E2M1[nib]
    vals = vals * np.repeat(np.exp2(scales.astype(np.float64) - 127.0), 8, axis=1)[..., None]
    return vals.transpose(0, 1, 3, 2).reshape(g * 512, n)

def planes(Y):
    n, m = Y.shape
    b = f64(bf(Y)).reshape(n // 32, 32, m)
    amax = np.abs(b).max(1)
    byte = np.clip(np.where(amax > 0, np.frexp(amax)[1] - 1 + 127 - 7, 1), 1, 254)
    codes = (b * np.exp2(127.0 - byte)[:, None, :]).reshape(n, m).astype(np.float32).astype(ml_dtypes.float8_e4m3fn).view(np.uint8)
    words = codes.reshape(n // 512, 128, 4, m).transpose(0, 1, 3, 2)
    return np.ascontiguousarray(words), np.ascontiguousarray(byte.astype(np.uint8).reshape(n // 512, 16, m))


Q, D, C, P = 1024, 512, 128, 4096


def sigmoid(v):
    return 1.0 / (1.0 + np.exp(-v))


def object_class_probs(z, u):
    mx = np.maximum(np.max(z, axis=1), u)
    e = np.exp(z - mx[:, None])
    e_void = np.exp(u - mx)
    denom = np.sum(e, axis=1) + e_void
    return e / denom[:, None]


def setup_inputs():
    a, b = mx_kscale(D), mx_kscale(D)
    t = mx_kscale(Q)
    sc = 2.0 / np.sqrt(D)
    emb = bf(np.random.standard_normal((Q, D)) * sc * a)
    pix = bf(np.random.standard_normal((P, D)) / a)
    queries = bf(np.random.standard_normal((Q, D)) * b)
    w_cls_words, w_cls_scales = pack_weight(np.random.standard_normal((D, C)) * sc / b[:, None], "e4m3")
    return {
        "emb": emb,
        "pix": pix,
        "queries": queries,
        "w_cls_words": w_cls_words,
        "w_cls_scales": w_cls_scales,
        "w_void": bf(np.random.standard_normal(D) * sc / b),
        "g_mask": bf((1.0 + 0.1 * np.random.standard_normal(Q)) / t),
        "g_cls": bf((1.0 + 0.1 * np.random.standard_normal(Q)) * t),
    }


def core(emb, pix, queries, w_cls_words, w_cls_scales, w_void, g_mask, g_cls):
    l = mxq(f64(emb), 1, "e4m3") @ mxq(f64(pix).T, 0, "e4m3")
    m = (sigmoid(l) - 0.5) * f64(g_mask)[:, None]
    z = mxq(f64(queries), 1, "e4m3") @ unpack_weight(w_cls_words, w_cls_scales, "e4m3")
    u = 6.0 + np.sum(f64(queries) * f64(w_void)[None, :], axis=1)
    prob = object_class_probs(z, u)
    s = (prob - np.mean(prob, axis=1, keepdims=True)) * f64(g_cls)[:, None]
    return mxq(s.T, 1, "e4m3") @ mxq(m, 0, "e4m3")


def reference(emb, pix, queries, w_cls_words, w_cls_scales, w_void, g_mask, g_cls):
    R_out = core(emb, pix, queries, w_cls_words, w_cls_scales, w_void, g_mask, g_cls)
    words, scales = planes(R_out.T)
    return R_out, words, scales

@@ -1,0 +1,415 @@
+from contextlib import ExitStack
+
+import concourse.mybir as mybir
+from concourse.masks import make_identity
+
+Q, D, C, NPIX = 1024, 512, 128, 4096
+P = 128
+FLOPS = 2 * Q * D * NPIX + 2 * Q * D * C + 2 * C * Q * NPIX
+
+F32 = mybir.dt.float32
+BF16 = mybir.dt.bfloat16
+U32 = mybir.dt.uint32
+I32 = mybir.dt.int32
+U8 = mybir.dt.uint8
+FP8X4 = mybir.dt.float8_e4m3fn_x4
+ACT = mybir.ActivationFunctionType
+ALU = mybir.AluOpType
+AX = mybir.AxisListType
+
+CHUNKS = NPIX // 512
+TICKS = 2 * CHUNKS
+
+
+def tile_maskquerysemanticinference_x2_kernel(
+    tc, emb, pix, queries, w_cls_words, w_cls_scales, w_void, g_mask, g_cls, out_0, out_1, out_2
+):
+    nc = tc.nc
+    with ExitStack() as ctx:
+        const = ctx.enter_context(tc.tile_pool(name="const", bufs=1))
+        raws = ctx.enter_context(tc.tile_pool(name="raws", bufs=1))
+        work = ctx.enter_context(tc.tile_pool(name="work", bufs=3))
+        psum = ctx.enter_context(tc.psum_pool(name="psum", bufs=1))
+        ctx.enter_context(tc.manual_schedule())
+
+        wcls = const.tile([P, P], U32, name="wcls", align_bytes=64)
+        wcls_sc = const.tile([P, P], U8, name="wcls_sc", align_bytes=64)
+        wv = const.tile([P, 4], BF16, name="wv", align_bytes=64)
+        gm16 = const.tile([P, 2, 4], BF16, name="gm16", align_bytes=64)
+        gc16 = const.tile([P, 2, 4], BF16, name="gc16", align_bytes=64)
+        ident = const.tile([P, P], F32, name="ident", align_bytes=64)
+        warm = const.tile([P, 1], F32, name="warm", align_bytes=64)
+
+        nc.vector.memset(warm[:], 0.0)
+        nc.vector.memset(wcls_sc[:].bitcast(I32), 0)
+        make_identity(nc, ident[:])
+
+        raw = {}
+
+        def load(src, idx, tag, pieces):
+            t = raws.tile([P, 4, D], BF16, name=f"raw_{tag}{idx}", tag=f"raw_{tag}{idx}", align_bytes=64)
+            view = src.rearrange("(g m t) k -> g m t k", m=P, t=4)[idx]
+            n = 4 // pieces
+            for h in range(pieces):
+                nc.sync.dma_start(out=t[:, n * h : n * h + n, :], in_=view[:, n * h : n * h + n, :])
+            raw[tag, idx] = t
+
+        load(emb, 0, "e", 2)
+        load(pix, 0, "p", 2)
+        load(emb, 1, "e", 2)
+        nc.scalar.dma_start(out=gm16[:], in_=g_mask.rearrange("(g p t) -> p g t", p=P, t=4))
+        nc.scalar.dma_start(out=wv[:], in_=w_void.rearrange("(p t) -> p t", t=4))
+        nc.scalar.dma_start(out=gc16[:], in_=g_cls.rearrange("(g p t) -> p g t", p=P, t=4))
+        nc.scalar.dma_start(out=wcls[:].bitcast(I32), in_=w_cls_words[0].rearrange("p n t -> p (n t)").bitcast(I32))
+        for b in range(4):
+            nc.scalar.dma_start(
+                out=wcls_sc[32 * b : 32 * b + 4, :].bitcast(I32), in_=w_cls_scales[0, 4 * b : 4 * b + 4, :].bitcast(I32)
+            )
+        load(pix, 1, "p", 1)
+        load(queries, 0, "q", 1)
+        load(queries, 1, "q", 1)
+        for c in range(2, CHUNKS):
+            load(pix, c, "p", 1)
+
+        nc.scalar.activation(out=warm[:], in_=warm[:], func=ACT.Exp)
+
+        gmh = const.tile([P, 2, 4], F32, name="gmh", align_bytes=64)
+        gcf = const.tile([P, 2, 4], F32, name="gcf", align_bytes=64)
+
+        def gains():
+            nc.vector.tensor_scalar(out=gmh[:], in0=gm16[:], scalar1=0.5, scalar2=None, op0=ALU.mult)
+            nc.vector.tensor_copy(out=gcf[:], in_=gc16[:])
+
+        BUFS = {"L": 4, "T": 2, "O": 2}
+
+        def bank(shape, tag):
+            t = psum.tile(shape, F32, name=f"bank_{tag}", tag=tag, bufs=BUFS[tag])
+            return t
+
+        banks, grouped, codes, scales = {}, {}, {}, {}
+
+        def turn(what, half, tag):
+            b = bank([P, 2, 2, P], tag)
+            for s in range(2):
+                words = raw[what][:, 2 * half + s, :].bitcast(F32)
+                for u in range(2):
+                    nc.tensor.transpose(b[:, s, u, :], words[:, u : D // 2 : 2], ident[:])
+            banks[what, half] = b
+
+        def group_tile(what):
+            if what not in grouped:
+                tag = "grp_" + what[0]
+                g = work.tile([P, 512, 4], BF16, name=tag, tag=tag, bufs=2, align_bytes=64)
+                grouped[what] = g
+            return grouped[what]
+
+        def copy(eng, out, in_):
+            if eng == "S":
+                nc.scalar.copy(out=out, in_=in_)
+            else:
+                nc.vector.tensor_copy(out=out, in_=in_)
+
+        def fetch(eng, what, half):
+            dst = group_tile(what)[:, 256 * half : 256 * half + 256, :].bitcast(F32)
+            copy(eng, dst.rearrange("p (s m) u -> p s m u", s=2), banks[what, half][:].rearrange("p s u m -> p s m u"))
+
+        def quant(what, part=None):
+            if what not in codes:
+                tag = what[0]
+                bufs = 3 if tag == "p" else 2
+                cd = work.tile([P, 512], U32, name="cd_" + tag, tag="cd_" + tag, bufs=bufs, align_bytes=64)
+                sc = work.tile([P, 512], U8, name="sc_" + tag, tag="sc_" + tag, bufs=bufs, align_bytes=64)
+                codes[what], scales[what] = cd, sc
+            cols = slice(0, 512) if part is None else slice(256 * part, 256 * part + 256)
+            nc.vector.quantize_mx(
+                out=codes[what][:, cols].bitcast(FP8X4),
+                scales=scales[what][:, cols],
+                in_=grouped[what][:, cols, :].rearrange("p c t -> p (c t)"),
+            )
+
+        def mx(out, a, a_sc, b, b_sc, start, stop):
+            nc.tensor.matmul_mx(
+                out=out, lhsT=a.bitcast(FP8X4), lhsT_scale=a_sc, rhs=b.bitcast(FP8X4), rhs_scale=b_sc, start=start, stop=stop
+            )
+
+        lbank, th, mb = {}, {}, {}
+
+        def logits(h, j):
+            c, g = divmod(h, 2)
+            b = bank([P, 4, P], "L")
+            px = slice(P * j, P * j + P)
+            for t in range(4):
+                qs = slice(P * t, P * t + P)
+                mx(b[:, t, :], codes["e", g][:, qs], scales["e", g][:, qs], codes["p", c][:, px], scales["p", c][:, px], True, True)
+            lbank[h, j] = b
+
+        def tanh(h, j):
+            if h not in th:
+                t = work.tile([P, 512, 4], F32, name="th", tag="th", bufs=3, align_bytes=64)
+                th[h] = t
+            nc.scalar.activation(
+                out=th[h][:, P * j : P * j + P, :], in_=lbank[h, j][:].rearrange("p t n -> p n t"), func=ACT.Tanh, scale=0.5
+            )
+
+        def gain(h, j0, n):
+            if h not in mb:
+                t = work.tile([P, 512, 4], BF16, name="mb", tag="mb", bufs=3, align_bytes=64)
+                mb[h] = t
+            cols = slice(P * j0, P * (j0 + n))
+            nc.vector.tensor_tensor(
+                out=mb[h][:, cols, :],
+                in0=th[h][:, cols, :],
+                in1=gmh[:, h % 2, :].unsqueeze(1).to_broadcast([P, P * n, 4]),
+                op=ALU.mult,
+            )
+
+        mc, ms = {}, {}
+
+        def quant_m(h, j=None):
+            if h not in mc:
+                a = work.tile([P, 512], U32, name="mc", tag="mc", bufs=10, align_bytes=64)
+                b = work.tile([P, 512], U8, name="ms", tag="ms", bufs=10, align_bytes=64)
+                mc[h], ms[h] = a, b
+            cols = slice(0, 512) if j is None else slice(P * j, P * j + P)
+            nc.vector.quantize_mx(
+                out=mc[h][:, cols].bitcast(FP8X4),
+                scales=ms[h][:, cols],
+                in_=mb[h][:, cols, :].rearrange("p c t -> p (c t)"),
+            )
+
+        small = {}
+
+        def col8(name):
+            if name not in small:
+                t = const.tile([P, 2, 4], F32, name=name, align_bytes=64)
+                small[name] = t
+            return small[name]
+
+        zbank, ubank = {}, {}
+
+        def class_logits(g):
+            b = bank([P, 4, P], "O")
+            for t in range(4):
+                qs = slice(P * t, P * t + P)
+                mx(b[:, t, :], codes["q", g][:, qs], scales["q", g][:, qs], wcls[:], wcls_sc[:], True, True)
+            zbank[g] = b
+
+        def void_logits():
+            b = bank([P, 2, 4], "T")
+            for g in range(2):
+                for t in range(4):
+                    for s in range(4):
+                        nc.tensor.matmul(
+                            b[:, g, t : t + 1],
+                            lhsT=grouped["q", g][:, P * t : P * t + P, s],
+                            rhs=wv[:, s : s + 1],
+                            start=(s == 0),
+                            stop=(s == 3),
+                        )
+            ubank[0] = b
+
+        def softmax_max():
+            u6, zm, nmx, ud = col8("u6"), col8("zm"), col8("nmx"), col8("ud")
+            nc.vector.tensor_scalar(out=u6[:], in0=ubank[0][:], scalar1=6.0, scalar2=None, op0=ALU.add)
+            for g in range(2):
+                nc.vector.tensor_reduce(out=zm[:, g, :], in_=zbank[g][:], axis=AX.X, op=ALU.max)
+            nc.vector.tensor_tensor(out=zm[:], in0=zm[:], in1=u6[:], op=ALU.max)
+            nc.vector.tensor_scalar(out=nmx[:], in0=zm[:], scalar1=-1.0, scalar2=None, op0=ALU.mult)
+            nc.vector.tensor_tensor(out=ud[:], in0=u6[:], in1=zm[:], op=ALU.subtract)
+
+        ez = const.tile([P, 2, 4, P], F32, name="ez", align_bytes=64)
+        sb = const.tile([P, 2, P, 4], BF16, name="sb", align_bytes=64)
+        s_cd = const.tile([P, 2, P], U32, name="s_cd", align_bytes=64)
+        s_sc = const.tile([P, 2, P], U8, name="s_sc", align_bytes=64)
+
+        def softmax_exp():
+            rs, ev = col8("rs"), col8("ev")
+            nmx, ud = col8("nmx"), col8("ud")
+            nc.scalar.activation(out=ev[:], in_=ud[:], func=ACT.Exp)
+            for g in range(2):
+                for t in range(4):
+                    nc.scalar.activation(
+                        out=ez[:, g, t, :],
+                        in_=zbank[g][:, t, :],
+                        func=ACT.Exp,
+                        bias=nmx[:, g, t : t + 1],
+                        accum_out=rs[:, g, t : t + 1],
+                    )
+
+        def softmax_scores():
+            rs, ev, den, rg, mean = col8("rs"), col8("ev"), col8("den"), col8("rg"), col8("mean")
+            nc.vector.tensor_tensor(out=den[:], in0=rs[:], in1=ev[:], op=ALU.add)
+            nc.vector.tensor_scalar(out=mean[:], in0=rs[:], scalar1=1.0 / C, scalar2=None, op0=ALU.mult)
+            nc.vector.reciprocal(out=den[:], in_=den[:])
+            nc.vector.tensor_tensor(out=rg[:], in0=den[:], in1=gcf[:], op=ALU.mult)
+            for g in range(2):
+                for t in range(4):
+                    nc.vector.tensor_scalar(
+                        out=sb[:, g, :, t],
+                        in0=ez[:, g, t, :],
+                        scalar1=mean[:, g, t : t + 1],
+                        scalar2=rg[:, g, t : t + 1],
+                        op0=ALU.subtract,
+                        op1=ALU.mult,
+                    )
+
+        def quant_s():
+            nc.vector.quantize_mx(
+                out=s_cd[:].rearrange("p g c -> p (g c)").bitcast(FP8X4),
+                scales=s_sc[:].rearrange("p g c -> p (g c)"),
+                in_=sb[:].rearrange("p g c t -> p (g c t)"),
+            )
+
+        obank, pbank = {}, {}
+        p_sc = const.tile([P, CHUNKS, P], U8, name="p_sc", align_bytes=64)
+        pg, pcd = {}, {}
+
+        def result_banks(c):
+            obank[c] = bank([P, 512], "O")
+            pbank[c] = bank([P, 4, P], "O")
+
+        def product(c):
+            for g in range(2):
+                h = 2 * c + g
+                mx(obank[c][:], s_cd[:, g, :], s_sc[:, g, :], mc[h][:], ms[h][:], g == 0, g == 1)
+            for j in range(4):
+                product_t(c, j)
+
+        def product_t(c, j):
+            px = slice(P * j, P * j + P)
+            for g in range(2):
+                h = 2 * c + g
+                mx(pbank[c][:, j, :], mc[h][:, px], ms[h][:, px], s_cd[:, g, :], s_sc[:, g, :], g == 0, g == 1)
+
+        def product_j(c, j):
+            px = slice(P * j, P * j + P)
+            for g in range(2):
+                h = 2 * c + g
+                mx(obank[c][:, px], s_cd[:, g, :], s_sc[:, g, :], mc[h][:, px], ms[h][:, px], g == 0, g == 1)
+            product_t(c, j)
+
+        def store_out(eng, c):
+            t = work.tile([P, P, 4], F32, name="res", tag="res", bufs=2, align_bytes=64)
+            copy(eng, t[:], obank[c][:].rearrange("p (j n) -> p n j", j=4))
+            nc.sync.dma_start(out=out_0[:, 512 * c : 512 * c + 512], in_=t[:].rearrange("p n j -> p (n j)"))
+
+        def fetch_p(eng, c):
+            t = work.tile([P, P, 4], BF16, name="pg", tag="pg", bufs=2, align_bytes=64)
+            copy(eng, t[:], pbank[c][:].rearrange("p j m -> p m j"))
+            pg[c] = t
+
+        def quant_p(c):
+            t = work.tile([P, P], U32, name="pcd", tag="pcd", bufs=2, align_bytes=64)
+            nc.vector.quantize_mx(
+                out=t[:].bitcast(FP8X4), scales=p_sc[:, c, :], in_=pg[c][:].rearrange("p m j -> p (m j)")
+            )
+            nc.sync.dma_start(out=out_1[c].rearrange("p m t -> p (m t)").bitcast(I32), in_=t[:].bitcast(I32))
+
+        def store_scales(c0, c1):
+            for b in range(4):
+                nc.sync.dma_start(
+                    out=out_2[c0:c1, 4 * b : 4 * b + 4, :].rearrange("c r m -> r c m").bitcast(I32),
+                    in_=p_sc[32 * b : 32 * b + 4, c0:c1, :].bitcast(I32),
+                )
+
+        E0, E1, P0, P1, Q0, Q1 = ("e", 0), ("e", 1), ("p", 0), ("p", 1), ("q", 0), ("q", 1)
+        turn(E0, 0, "T")
+        turn(E0, 1, "T")
+        turn(P0, 0, "O")
+        turn(P0, 1, "O")
+        fetch("S", E0, 0)
+        fetch("V", E0, 1)
+        quant(E0, 0)
+        quant(E0, 1)
+        fetch("S", P0, 0)
+        fetch("V", P0, 1)
+        quant(P0, 0)
+        quant(P0, 1)
+        gains()
+
+        PX = {c: ("p", c) for c in range(CHUNKS)}
+        turns = {0: [(E1, 0, "T"), (E1, 1, "T"), (P1, 0, "O"), (P1, 1, "O")], 1: [(Q0, 0, "T"), (Q0, 1, "T")], 2: [(Q1, 0, "T"), (Q1, 1, "T"), (2, 0, "O"), (2, 1, "O")], 3: [(3, 0, "T")], 4: [(3, 1, "T")], 5: [(4, 0, "T")], 6: [(4, 1, "T")], 7: [(5, 0, "T")], 8: [(5, 1, "T")], 9: [(6, 0, "T")], 10: [(6, 1, "T")], 11: [(7, 0, "T")], 12: [(7, 1, "T")]}
+        sA = {1: [("f", Q0, 0)], 2: [("f", Q1, 0)], 3: [("f", 3, 0)], 4: [("f", 3, 1)], 5: [("sexp",), ("f", 4, 0)], 6: [("f", 4, 1)], 7: [("f", 5, 0)], 8: [("f", 5, 1)], 9: [("f", 6, 0)], 10: [("f", 6, 1)], 11: [("f", 7, 0)], 12: [("f", 7, 1)]}
+        sB = {0: [("f", P1, 0), ("f", P1, 1)], 2: [("f", 2, 0), ("f", 2, 1)], 7: [("P", 0), ("o", 0)], 8: [("P", 1), ("o", 1)], 9: [("P", 2), ("o", 2)], 10: [("P", 3), ("o", 3)], 11: [("P", 4), ("o", 4)], 13: [("P", 5), ("o", 5)], 15: [("P", 6), ("o", 6)]}
+        vA = {1: [("f", Q0, 1)], 2: [("f", Q1, 1)], 4: [("smax",)], 6: [("ssc",)]}
+        vB = {0: [("q", P1)], 1: [("q", Q0)], 2: [("q", Q1), ("q", 2)], 4: [("q", 3)], 6: [("qs",), ("q", 4)], 8: [("q", 5), ("qp", 0)], 9: [("qp", 1)], 10: [("q", 6), ("qp", 2)], 11: [("qp", 3)], 12: [("q", 7), ("qp", 4)], 14: [("qp", 5)], 15: [("qp", 6)]}
+        products = {7: [0], 8: [1], 9: [2], 10: [3], 11: [4], 13: [5], 15: [6]}
+        zu = 4
+
+        def run(eng, item):
+            kind = item[0]
+            if kind == "f":
+                fetch(eng, PX[item[1]] if isinstance(item[1], int) else item[1], item[2])
+            elif kind == "q":
+                quant(PX[item[1]] if isinstance(item[1], int) else item[1])
+            elif kind == "o":
+                store_out(eng, item[1])
+            elif kind == "P":
+                fetch_p(eng, item[1])
+            elif kind == "qp":
+                quant_p(item[1])
+            elif kind == "smax":
+                softmax_max()
+            elif kind == "sexp":
+                softmax_exp()
+            elif kind == "ssc":
+                softmax_scores()
+            elif kind == "qs":
+                quant_s()
+
+        for h in range(TICKS):
+            last = h == TICKS - 1
+            for j in range(4):
+                logits(h, j)
+            for what, half, tag in turns.get(h, []):
+                turn(PX[what] if isinstance(what, int) else what, half, tag)
+            if h == zu:
+                class_logits(0)
+                class_logits(1)
+                void_logits()
+            for c in products.get(h, []):
+                result_banks(c)
+                product(c)
+            tanh(h, 0)
+            tanh(h, 1)
+            for it in sA.get(h, []):
+                run("S", it)
+            tanh(h, 2)
+            tanh(h, 3)
+            for it in sB.get(h, []):
+                run("S", it)
+            if not last:
+                for it in {0: [("f", E1, 0), ("f", E1, 1), ("q", E1)]}.get(h, []):
+                    run("V", it)
+                gain(h, 0, 2)
+                if h > 0:
+                    quant_m(h - 1)
+                for it in vA.get(h, []):
+                    run("V", it)
+                gain(h, 2, 2)
+                for it in vB.get(h, []):
+                    run("V", it)
+            else:
+                gain(h, 0, 1)
+                quant_m(h - 1)
+                for it in vA.get(h, []):
+                    run("V", it)
+                gain(h, 1, 1)
+                quant_m(h, 0)
+                gain(h, 2, 1)
+                quant_m(h, 1)
+                gain(h, 3, 1)
+                quant_m(h, 2)
+                for it in vB.get(h, []):
+                    run("V", it)
+                quant_m(h, 3)
+
+        c = CHUNKS - 1
+        store_scales(0, c)
+        result_banks(c)
+        for j in range(4):
+            product_j(c, j)
+        fetch_p("V", c)
+        store_out("S", c)
+        quant_p(c)
+        store_scales(c, c + 1)

@@ -21,6 +21,9 @@ CHUNKS = NPIX // 512
 TICKS = 2 * CHUNKS
 
 
+PLAN = {'pe': {(1, 3): [('t', ('p', 2), 0, 'O')], (15, 1): [('pr', 6)], (1, 4): [('t', ('q', 0), 1, 'T')], (-1, 4): [('t', ('e', 0), 1, 'T'), ('t', ('p', 0), 0, 'O'), ('t', ('p', 0), 1, 'O')], (0, 0): [('t', ('e', 1), 0, 'O'), ('t', ('e', 1), 1, 'T')], (2, 4): [('t', ('p', 3), 0, 'O')], (12, 2): [('t', ('p', 7), 0, 'T')], (6, 1): [('t', ('p', 4), 1, 'T')], (1, 1): [('t', ('q', 0), 0, 'O')], (3, 4): [('t', ('p', 3), 1, 'T')], (10, 0): [('t', ('p', 6), 1, 'T')], (-1, 0): [('t', ('e', 0), 0, 'T')], (12, 3): [('t', ('p', 7), 1, 'T')], (10, 3): [('pr', 3)], (9, 3): [('pr', 2)], (4, 2): [('z',)], (10, 2): [('t', ('p', 6), 0, 'T')], (5, 0): [('t', ('p', 4), 0, 'T')], (14, 0): [('pr', 5)], (9, 0): [('pr', 1)], (3, 1): [('t', ('q', 1), 1, 'T')], (2, 2): [('t', ('p', 2), 1, 'O')], (7, 4): [('pr', 0)], (0, 2): [('t', ('p', 1), 0, 'T'), ('t', ('p', 1), 1, 'O')], (2, 3): [('t', ('q', 1), 0, 'T')], (8, 0): [('t', ('p', 5), 1, 'T')], (11, 1): [('pr', 4)], (6, 2): [('t', ('p', 5), 0, 'O')]}, 's': {(12, 2): [('f', ('p', 7), 0)], (14, 3): [('P', 5)], (0, 3): [('f', ('p', 1), 1)], (5, 2): [('sexp',), ('f', ('p', 4), 0)], (4, 1): [('f', ('p', 3), 1)], (8, 4): [('f', ('p', 5), 1)], (8, 0): [('o', 0), ('P', 0)], (6, 2): [('f', ('p', 5), 0)], (10, 2): [('f', ('p', 6), 1), ('P', 3), ('f', ('p', 6), 0)], (15, 1): [('o', 6)], (14, 1): [('o', 5)], (-1, 6): [('f', ('p', 0), 1)], (9, 0): [('P', 1), ('o', 1)], (0, 0): [('f', ('e', 1), 0)], (-1, 4): [('f', ('e', 0), 1)], (2, 4): [('f', ('q', 0), 1), ('f', ('q', 1), 0)], (11, 1): [('o', 4)], (-1, 2): [('f', ('p', 0), 0)], (3, 2): [('f', ('q', 1), 1)], (6, 3): [('f', ('p', 4), 1)], (2, 0): [('f', ('p', 2), 0)], (9, 1): [('o', 2)], (3, 3): [('f', ('p', 3), 0)], (9, 4): [('P', 2)], (2, 1): [('f', ('p', 2), 1)], (12, 4): [('f', ('p', 7), 1)], (15, 3): [('P', 6)], (13, 0): [('P', 4)], (1, 2): [('f', ('q', 0), 0)]}, 'v': {(0, 1): [('f', ('p', 1), 0)], (10, 0): [('o', 3)], (8, 0): [('qp', 0)], (14, 1): [('qp', 5)], (4, 0): [('q', ('p', 3))], (0, 0): [('f', ('e', 1), 1), ('gains',), ('q', ('e', 1))], (9, 2): [('qp', 1)], (10, 1): [('q', ('p', 6))], (2, 1): [('q', ('p', 2)), ('q', ('q', 0))], (-1, 11): [('qh', ('p', 0), 1)], (-1, 3): [('f', ('e', 0), 0)], (-1, 4): [('qh', ('p', 0), 0)], (8, 2): [('q', ('p', 5))], (5, 1): [('ssc',)], (3, 0): [('q', ('q', 1))], (0, 2): [('q', ('p', 1))], (5, 2): [('qs',)], (4, 1): [('smax',)], (13, 0): [('qp', 3)], (15, 2): [('qp', 6)], (-1, 9): [('qh', ('e', 0), 1)], (6, 0): [('q', ('p', 4))], (9, 1): [('qp', 2)], (-1, 6): [('qh', ('e', 0), 0)], (13, 1): [('qp', 4)], (12, 1): [('q', ('p', 7))]}, 'W': 0, 'GP': 64}
+
+
 def tile_maskquerysemanticinference_x2_kernel(
     tc, emb, pix, queries, w_cls_words, w_cls_scales, w_void, g_mask, g_cls, out_0, out_1, out_2
 ):
@@ -76,9 +79,11 @@ def tile_maskquerysemanticinference_x2_kernel(
         gmh = const.tile([P, 2, 4], F32, name="gmh", align_bytes=64)
         gcf = const.tile([P, 2, 4], F32, name="gcf", align_bytes=64)
 
+
         def gains():
-            nc.vector.tensor_scalar(out=gmh[:], in0=gm16[:], scalar1=0.5, scalar2=None, op0=ALU.mult)
-            nc.vector.tensor_copy(out=gcf[:], in_=gc16[:])
+            nc.gpsimd.tensor_scalar(out=gmh[:], in0=gm16[:], scalar1=0.5, scalar2=None, op0=ALU.mult)
+            nc.gpsimd.tensor_copy(out=gcf[:], in_=gc16[:])
+
 
         BUFS = {"L": 4, "T": 2, "O": 2}
 
@@ -151,15 +156,15 @@ def tile_maskquerysemanticinference_x2_kernel(
                 out=th[h][:, P * j : P * j + P, :], in_=lbank[h, j][:].rearrange("p t n -> p n t"), func=ACT.Tanh, scale=0.5
             )
 
-        def gain(h, j0, n):
+        def gain(eng, h, c0, c1):
             if h not in mb:
                 t = work.tile([P, 512, 4], BF16, name="mb", tag="mb", bufs=3, align_bytes=64)
                 mb[h] = t
-            cols = slice(P * j0, P * (j0 + n))
-            nc.vector.tensor_tensor(
-                out=mb[h][:, cols, :],
-                in0=th[h][:, cols, :],
-                in1=gmh[:, h % 2, :].unsqueeze(1).to_broadcast([P, P * n, 4]),
+            src = gmh
+            eng.tensor_tensor(
+                out=mb[h][:, c0:c1, :],
+                in0=th[h][:, c0:c1, :],
+                in1=src[:, h % 2, :].unsqueeze(1).to_broadcast([P, c1 - c0, 4]),
                 op=ALU.mult,
             )
 
@@ -214,10 +219,11 @@ def tile_maskquerysemanticinference_x2_kernel(
             for g in range(2):
                 nc.vector.tensor_reduce(out=zm[:, g, :], in_=zbank[g][:], axis=AX.X, op=ALU.max)
             nc.vector.tensor_tensor(out=zm[:], in0=zm[:], in1=u6[:], op=ALU.max)
-            nc.vector.tensor_scalar(out=nmx[:], in0=zm[:], scalar1=-1.0, scalar2=None, op0=ALU.mult)
-            nc.vector.tensor_tensor(out=ud[:], in0=u6[:], in1=zm[:], op=ALU.subtract)
+            nc.gpsimd.tensor_scalar(out=nmx[:], in0=zm[:], scalar1=-1.0, scalar2=None, op0=ALU.mult)
+            nc.gpsimd.tensor_tensor(out=ud[:], in0=u6[:], in1=zm[:], op=ALU.subtract)
 
         ez = const.tile([P, 2, 4, P], F32, name="ez", align_bytes=64)
+        sflat = const.tile([P, 2, 4, P], BF16, name="sflat", align_bytes=64)
         sb = const.tile([P, 2, P, 4], BF16, name="sb", align_bytes=64)
         s_cd = const.tile([P, 2, P], U32, name="s_cd", align_bytes=64)
         s_sc = const.tile([P, 2, P], U8, name="s_sc", align_bytes=64)
@@ -238,20 +244,21 @@ def tile_maskquerysemanticinference_x2_kernel(
 
         def softmax_scores():
             rs, ev, den, rg, mean = col8("rs"), col8("ev"), col8("den"), col8("rg"), col8("mean")
-            nc.vector.tensor_tensor(out=den[:], in0=rs[:], in1=ev[:], op=ALU.add)
-            nc.vector.tensor_scalar(out=mean[:], in0=rs[:], scalar1=1.0 / C, scalar2=None, op0=ALU.mult)
+            nc.gpsimd.tensor_tensor(out=den[:], in0=rs[:], in1=ev[:], op=ALU.add)
+            nc.gpsimd.tensor_scalar(out=mean[:], in0=rs[:], scalar1=1.0 / C, scalar2=None, op0=ALU.mult)
             nc.vector.reciprocal(out=den[:], in_=den[:])
-            nc.vector.tensor_tensor(out=rg[:], in0=den[:], in1=gcf[:], op=ALU.mult)
+            nc.gpsimd.tensor_tensor(out=rg[:], in0=den[:], in1=gcf[:], op=ALU.mult)
             for g in range(2):
                 for t in range(4):
                     nc.vector.tensor_scalar(
-                        out=sb[:, g, :, t],
+                        out=sflat[:, g, t, :],
                         in0=ez[:, g, t, :],
                         scalar1=mean[:, g, t : t + 1],
                         scalar2=rg[:, g, t : t + 1],
                         op0=ALU.subtract,
                         op1=ALU.mult,
                     )
+                nc.vector.tensor_copy(out=sb[:, g, :, :], in_=sflat[:, g, :, :].rearrange("p t c -> p c t"))
 
         def quant_s():
             nc.vector.quantize_mx(
@@ -312,104 +319,86 @@ def tile_maskquerysemanticinference_x2_kernel(
                     in_=p_sc[32 * b : 32 * b + 4, c0:c1, :].bitcast(I32),
                 )
 
-        E0, E1, P0, P1, Q0, Q1 = ("e", 0), ("e", 1), ("p", 0), ("p", 1), ("q", 0), ("q", 1)
-        turn(E0, 0, "T")
-        turn(E0, 1, "T")
-        turn(P0, 0, "O")
-        turn(P0, 1, "O")
-        fetch("S", E0, 0)
-        fetch("V", E0, 1)
-        quant(E0, 0)
-        quant(E0, 1)
-        fetch("S", P0, 0)
-        fetch("V", P0, 1)
-        quant(P0, 0)
-        quant(P0, 1)
-        gains()
+        def key(w):
+            return (w[0], w[1])
 
-        PX = {c: ("p", c) for c in range(CHUNKS)}
-        turns = {0: [(E1, 0, "T"), (E1, 1, "T"), (P1, 0, "O"), (P1, 1, "O")], 1: [(Q0, 0, "T"), (Q0, 1, "T")], 2: [(Q1, 0, "T"), (Q1, 1, "T"), (2, 0, "O"), (2, 1, "O")], 3: [(3, 0, "T")], 4: [(3, 1, "T")], 5: [(4, 0, "T")], 6: [(4, 1, "T")], 7: [(5, 0, "T")], 8: [(5, 1, "T")], 9: [(6, 0, "T")], 10: [(6, 1, "T")], 11: [(7, 0, "T")], 12: [(7, 1, "T")]}
-        sA = {1: [("f", Q0, 0)], 2: [("f", Q1, 0)], 3: [("f", 3, 0)], 4: [("f", 3, 1)], 5: [("sexp",), ("f", 4, 0)], 6: [("f", 4, 1)], 7: [("f", 5, 0)], 8: [("f", 5, 1)], 9: [("f", 6, 0)], 10: [("f", 6, 1)], 11: [("f", 7, 0)], 12: [("f", 7, 1)]}
-        sB = {0: [("f", P1, 0), ("f", P1, 1)], 2: [("f", 2, 0), ("f", 2, 1)], 7: [("P", 0), ("o", 0)], 8: [("P", 1), ("o", 1)], 9: [("P", 2), ("o", 2)], 10: [("P", 3), ("o", 3)], 11: [("P", 4), ("o", 4)], 13: [("P", 5), ("o", 5)], 15: [("P", 6), ("o", 6)]}
-        vA = {1: [("f", Q0, 1)], 2: [("f", Q1, 1)], 4: [("smax",)], 6: [("ssc",)]}
-        vB = {0: [("q", P1)], 1: [("q", Q0)], 2: [("q", Q1), ("q", 2)], 4: [("q", 3)], 6: [("qs",), ("q", 4)], 8: [("q", 5), ("qp", 0)], 9: [("qp", 1)], 10: [("q", 6), ("qp", 2)], 11: [("qp", 3)], 12: [("q", 7), ("qp", 4)], 14: [("qp", 5)], 15: [("qp", 6)]}
-        products = {7: [0], 8: [1], 9: [2], 10: [3], 11: [4], 13: [5], 15: [6]}
-        zu = 4
+        def run(eng, it):
+            k = it[0]
+            if k == "f": fetch(eng, it[1], it[2])
+            elif k == "q": quant(it[1])
+            elif k == "qh": quant(it[1], it[2])
+            elif k == "o": store_out(eng, it[1])
+            elif k == "P": fetch_p(eng, it[1])
+            elif k == "qp": quant_p(it[1])
+            elif k == "smax": softmax_max()
+            elif k == "sexp": softmax_exp()
+            elif k == "ssc": softmax_scores()
+            elif k == "qs": quant_s()
+            elif k == "gains":
+                gains()
 
-        def run(eng, item):
-            kind = item[0]
-            if kind == "f":
-                fetch(eng, PX[item[1]] if isinstance(item[1], int) else item[1], item[2])
-            elif kind == "q":
-                quant(PX[item[1]] if isinstance(item[1], int) else item[1])
-            elif kind == "o":
-                store_out(eng, item[1])
-            elif kind == "P":
-                fetch_p(eng, item[1])
-            elif kind == "qp":
-                quant_p(item[1])
-            elif kind == "smax":
-                softmax_max()
-            elif kind == "sexp":
-                softmax_exp()
-            elif kind == "ssc":
-                softmax_scores()
-            elif kind == "qs":
-                quant_s()
-
-        for h in range(TICKS):
-            last = h == TICKS - 1
-            for j in range(4):
-                logits(h, j)
-            for what, half, tag in turns.get(h, []):
-                turn(PX[what] if isinstance(what, int) else what, half, tag)
-            if h == zu:
-                class_logits(0)
-                class_logits(1)
-                void_logits()
-            for c in products.get(h, []):
+        for h in range(-1, TICKS + 1):
+            for pos in range(5):
+                if pos == 3 and 0 <= h < TICKS:
+                    for it in PLAN["s"].get((h, 0), []):
+                        run("S", it)
+                    tanh(h, 0)
+                for it in PLAN["pe"].get((h, pos), []):
+                    if it[0] == "t":
+                        turn(it[1], it[2], it[3])
+                    elif it[0] == "z":
+                        class_logits(0)
+                        class_logits(1)
+                        void_logits()
+                    elif it[0] == "pr":
+                        result_banks(it[1])
+                        product(it[1])
+                if pos < 4 and 0 <= h < TICKS:
+                    logits(h, pos)
+            if h == TICKS:
+                c = CHUNKS - 1
+                store_scales(0, c)
                 result_banks(c)
-                product(c)
-            tanh(h, 0)
-            tanh(h, 1)
-            for it in sA.get(h, []):
-                run("S", it)
-            tanh(h, 2)
-            tanh(h, 3)
-            for it in sB.get(h, []):
-                run("S", it)
-            if not last:
-                for it in {0: [("f", E1, 0), ("f", E1, 1), ("q", E1)]}.get(h, []):
-                    run("V", it)
-                gain(h, 0, 2)
-                if h > 0:
-                    quant_m(h - 1)
-                for it in vA.get(h, []):
-                    run("V", it)
-                gain(h, 2, 2)
-                for it in vB.get(h, []):
-                    run("V", it)
+                for j in range(4):
+                    product_j(c, j)
+                fetch_p("V", c)
+                store_out("S", c)
+                quant_p(c)
+                store_scales(c, c + 1)
+                continue
+            if h == -1:
+                for pos in range(12):
+                    for it in PLAN["s"].get((h, pos), []):
+                        run("S", it)
+                    for it in PLAN["v"].get((h, pos), []):
+                        run("V", it)
+                continue
+            for pos in range(1, 5):
+                for it in PLAN["s"].get((h, pos), []):
+                    run("S", it)
+                if pos < 4:
+                    tanh(h, pos)
+            V = PLAN["v"]
+            W = PLAN["W"] if h < TICKS - 1 else 0
+            for c0 in range(0, W, PLAN["GP"]):
+                gain(nc.gpsimd, h, c0, min(W, c0 + PLAN["GP"]))
+            if h < TICKS - 1:
+                for it in V.get((h, 0), []): run("V", it)
+                gain(nc.vector, h, W, 256)
+                if h > 0: quant_m(h - 1)
+                for it in V.get((h, 1), []): run("V", it)
+                gain(nc.vector, h, 256, 512)
+                for it in V.get((h, 2), []): run("V", it)
             else:
-                gain(h, 0, 1)
+                for it in V.get((h, 0), []): run("V", it)
+                gain(nc.vector, h, 0, 128)
                 quant_m(h - 1)
-                for it in vA.get(h, []):
-                    run("V", it)
-                gain(h, 1, 1)
+                for it in V.get((h, 1), []): run("V", it)
+                gain(nc.vector, h, 128, 256)
                 quant_m(h, 0)
-                gain(h, 2, 1)
+                gain(nc.vector, h, 256, 384)
                 quant_m(h, 1)
-                gain(h, 3, 1)
+                gain(nc.vector, h, 384, 512)
                 quant_m(h, 2)
-                for it in vB.get(h, []):
-                    run("V", it)
+                for it in V.get((h, 2), []): run("V", it)
                 quant_m(h, 3)
-
-        c = CHUNKS - 1
-        store_scales(0, c)
-        result_banks(c)
-        for j in range(4):
-            product_j(c, j)
-        fetch_p("V", c)
-        store_out("S", c)
-        quant_p(c)
-        store_scales(c, c + 1)

from contextlib import ExitStack

import concourse.mybir as mybir
from concourse.masks import make_identity

Q, D, C, NPIX = 1024, 512, 128, 4096
P = 128
FLOPS = 2 * Q * D * NPIX + 2 * Q * D * C + 2 * C * Q * NPIX

F32 = mybir.dt.float32
BF16 = mybir.dt.bfloat16
U32 = mybir.dt.uint32
I32 = mybir.dt.int32
U8 = mybir.dt.uint8
FP8X4 = mybir.dt.float8_e4m3fn_x4
ACT = mybir.ActivationFunctionType
ALU = mybir.AluOpType
AX = mybir.AxisListType

CHUNKS = NPIX // 512
TICKS = 2 * CHUNKS


PLAN = {'pe': {(1, 3): [('t', ('p', 2), 0, 'O')], (15, 1): [('pr', 6)], (1, 4): [('t', ('q', 0), 1, 'T')], (-1, 4): [('t', ('e', 0), 1, 'T'), ('t', ('p', 0), 0, 'O'), ('t', ('p', 0), 1, 'O')], (0, 0): [('t', ('e', 1), 0, 'O'), ('t', ('e', 1), 1, 'T')], (2, 4): [('t', ('p', 3), 0, 'O')], (12, 2): [('t', ('p', 7), 0, 'T')], (6, 1): [('t', ('p', 4), 1, 'T')], (1, 1): [('t', ('q', 0), 0, 'O')], (3, 4): [('t', ('p', 3), 1, 'T')], (10, 0): [('t', ('p', 6), 1, 'T')], (-1, 0): [('t', ('e', 0), 0, 'T')], (12, 3): [('t', ('p', 7), 1, 'T')], (10, 3): [('pr', 3)], (9, 3): [('pr', 2)], (4, 2): [('z',)], (10, 2): [('t', ('p', 6), 0, 'T')], (5, 0): [('t', ('p', 4), 0, 'T')], (14, 0): [('pr', 5)], (9, 0): [('pr', 1)], (3, 1): [('t', ('q', 1), 1, 'T')], (2, 2): [('t', ('p', 2), 1, 'O')], (7, 4): [('pr', 0)], (0, 2): [('t', ('p', 1), 0, 'T'), ('t', ('p', 1), 1, 'O')], (2, 3): [('t', ('q', 1), 0, 'T')], (8, 0): [('t', ('p', 5), 1, 'T')], (11, 1): [('pr', 4)], (6, 2): [('t', ('p', 5), 0, 'O')]}, 's': {(12, 2): [('f', ('p', 7), 0)], (14, 3): [('P', 5)], (0, 3): [('f', ('p', 1), 1)], (5, 2): [('sexp',), ('f', ('p', 4), 0)], (4, 1): [('f', ('p', 3), 1)], (8, 4): [('f', ('p', 5), 1)], (8, 0): [('o', 0), ('P', 0)], (6, 2): [('f', ('p', 5), 0)], (10, 2): [('f', ('p', 6), 1), ('P', 3), ('f', ('p', 6), 0)], (15, 1): [('o', 6)], (14, 1): [('o', 5)], (-1, 6): [('f', ('p', 0), 1)], (9, 0): [('P', 1), ('o', 1)], (0, 0): [('f', ('e', 1), 0)], (-1, 4): [('f', ('e', 0), 1)], (2, 4): [('f', ('q', 0), 1), ('f', ('q', 1), 0)], (11, 1): [('o', 4)], (-1, 2): [('f', ('p', 0), 0)], (3, 2): [('f', ('q', 1), 1)], (6, 3): [('f', ('p', 4), 1)], (2, 0): [('f', ('p', 2), 0)], (9, 1): [('o', 2)], (3, 3): [('f', ('p', 3), 0)], (9, 4): [('P', 2)], (2, 1): [('f', ('p', 2), 1)], (12, 4): [('f', ('p', 7), 1)], (15, 3): [('P', 6)], (13, 0): [('P', 4)], (1, 2): [('f', ('q', 0), 0)]}, 'v': {(0, 1): [('f', ('p', 1), 0)], (10, 0): [('o', 3)], (8, 0): [('qp', 0)], (14, 1): [('qp', 5)], (4, 0): [('q', ('p', 3))], (0, 0): [('f', ('e', 1), 1), ('gains',), ('q', ('e', 1))], (9, 2): [('qp', 1)], (10, 1): [('q', ('p', 6))], (2, 1): [('q', ('p', 2)), ('q', ('q', 0))], (-1, 11): [('qh', ('p', 0), 1)], (-1, 3): [('f', ('e', 0), 0)], (-1, 4): [('qh', ('p', 0), 0)], (8, 2): [('q', ('p', 5))], (5, 1): [('ssc',)], (3, 0): [('q', ('q', 1))], (0, 2): [('q', ('p', 1))], (5, 2): [('qs',)], (4, 1): [('smax',)], (13, 0): [('qp', 3)], (15, 2): [('qp', 6)], (-1, 9): [('qh', ('e', 0), 1)], (6, 0): [('q', ('p', 4))], (9, 1): [('qp', 2)], (-1, 6): [('qh', ('e', 0), 0)], (13, 1): [('qp', 4)], (12, 1): [('q', ('p', 7))]}, 'W': 0, 'GP': 64}


def tile_maskquerysemanticinference_x2_kernel(
    tc, emb, pix, queries, w_cls_words, w_cls_scales, w_void, g_mask, g_cls, out_0, out_1, out_2
):
    nc = tc.nc
    with ExitStack() as ctx:
        const = ctx.enter_context(tc.tile_pool(name="const", bufs=1))
        raws = ctx.enter_context(tc.tile_pool(name="raws", bufs=1))
        work = ctx.enter_context(tc.tile_pool(name="work", bufs=3))
        psum = ctx.enter_context(tc.psum_pool(name="psum", bufs=1))
        ctx.enter_context(tc.manual_schedule())

        wcls = const.tile([P, P], U32, name="wcls", align_bytes=64)
        wcls_sc = const.tile([P, P], U8, name="wcls_sc", align_bytes=64)
        wv = const.tile([P, 4], BF16, name="wv", align_bytes=64)
        gm16 = const.tile([P, 2, 4], BF16, name="gm16", align_bytes=64)
        gc16 = const.tile([P, 2, 4], BF16, name="gc16", align_bytes=64)
        ident = const.tile([P, P], F32, name="ident", align_bytes=64)
        warm = const.tile([P, 1], F32, name="warm", align_bytes=64)

        nc.vector.memset(warm[:], 0.0)
        nc.vector.memset(wcls_sc[:].bitcast(I32), 0)
        make_identity(nc, ident[:])

        raw = {}

        def load(src, idx, tag, pieces):
            t = raws.tile([P, 4, D], BF16, name=f"raw_{tag}{idx}", tag=f"raw_{tag}{idx}", align_bytes=64)
            view = src.rearrange("(g m t) k -> g m t k", m=P, t=4)[idx]
            n = 4 // pieces
            for h in range(pieces):
                nc.sync.dma_start(out=t[:, n * h : n * h + n, :], in_=view[:, n * h : n * h + n, :])
            raw[tag, idx] = t

        load(emb, 0, "e", 2)
        load(pix, 0, "p", 2)
        load(emb, 1, "e", 2)
        nc.scalar.dma_start(out=gm16[:], in_=g_mask.rearrange("(g p t) -> p g t", p=P, t=4))
        nc.scalar.dma_start(out=wv[:], in_=w_void.rearrange("(p t) -> p t", t=4))
        nc.scalar.dma_start(out=gc16[:], in_=g_cls.rearrange("(g p t) -> p g t", p=P, t=4))
        nc.scalar.dma_start(out=wcls[:].bitcast(I32), in_=w_cls_words[0].rearrange("p n t -> p (n t)").bitcast(I32))
        for b in range(4):
            nc.scalar.dma_start(
                out=wcls_sc[32 * b : 32 * b + 4, :].bitcast(I32), in_=w_cls_scales[0, 4 * b : 4 * b + 4, :].bitcast(I32)
            )
        load(pix, 1, "p", 1)
        load(queries, 0, "q", 1)
        load(queries, 1, "q", 1)
        for c in range(2, CHUNKS):
            load(pix, c, "p", 1)

        nc.scalar.activation(out=warm[:], in_=warm[:], func=ACT.Exp)

        gmh = const.tile([P, 2, 4], F32, name="gmh", align_bytes=64)
        gcf = const.tile([P, 2, 4], F32, name="gcf", align_bytes=64)


        def gains():
            nc.gpsimd.tensor_scalar(out=gmh[:], in0=gm16[:], scalar1=0.5, scalar2=None, op0=ALU.mult)
            nc.gpsimd.tensor_copy(out=gcf[:], in_=gc16[:])


        BUFS = {"L": 4, "T": 2, "O": 2}

        def bank(shape, tag):
            t = psum.tile(shape, F32, name=f"bank_{tag}", tag=tag, bufs=BUFS[tag])
            return t

        banks, grouped, codes, scales = {}, {}, {}, {}

        def turn(what, half, tag):
            b = bank([P, 2, 2, P], tag)
            for s in range(2):
                words = raw[what][:, 2 * half + s, :].bitcast(F32)
                for u in range(2):
                    nc.tensor.transpose(b[:, s, u, :], words[:, u : D // 2 : 2], ident[:])
            banks[what, half] = b

        def group_tile(what):
            if what not in grouped:
                tag = "grp_" + what[0]
                g = work.tile([P, 512, 4], BF16, name=tag, tag=tag, bufs=2, align_bytes=64)
                grouped[what] = g
            return grouped[what]

        def copy(eng, out, in_):
            if eng == "S":
                nc.scalar.copy(out=out, in_=in_)
            else:
                nc.vector.tensor_copy(out=out, in_=in_)

        def fetch(eng, what, half):
            dst = group_tile(what)[:, 256 * half : 256 * half + 256, :].bitcast(F32)
            copy(eng, dst.rearrange("p (s m) u -> p s m u", s=2), banks[what, half][:].rearrange("p s u m -> p s m u"))

        def quant(what, part=None):
            if what not in codes:
                tag = what[0]
                bufs = 3 if tag == "p" else 2
                cd = work.tile([P, 512], U32, name="cd_" + tag, tag="cd_" + tag, bufs=bufs, align_bytes=64)
                sc = work.tile([P, 512], U8, name="sc_" + tag, tag="sc_" + tag, bufs=bufs, align_bytes=64)
                codes[what], scales[what] = cd, sc
            cols = slice(0, 512) if part is None else slice(256 * part, 256 * part + 256)
            nc.vector.quantize_mx(
                out=codes[what][:, cols].bitcast(FP8X4),
                scales=scales[what][:, cols],
                in_=grouped[what][:, cols, :].rearrange("p c t -> p (c t)"),
            )

        def mx(out, a, a_sc, b, b_sc, start, stop):
            nc.tensor.matmul_mx(
                out=out, lhsT=a.bitcast(FP8X4), lhsT_scale=a_sc, rhs=b.bitcast(FP8X4), rhs_scale=b_sc, start=start, stop=stop
            )

        lbank, th, mb = {}, {}, {}

        def logits(h, j):
            c, g = divmod(h, 2)
            b = bank([P, 4, P], "L")
            px = slice(P * j, P * j + P)
            for t in range(4):
                qs = slice(P * t, P * t + P)
                mx(b[:, t, :], codes["e", g][:, qs], scales["e", g][:, qs], codes["p", c][:, px], scales["p", c][:, px], True, True)
            lbank[h, j] = b

        def tanh(h, j):
            if h not in th:
                t = work.tile([P, 512, 4], F32, name="th", tag="th", bufs=3, align_bytes=64)
                th[h] = t
            nc.scalar.activation(
                out=th[h][:, P * j : P * j + P, :], in_=lbank[h, j][:].rearrange("p t n -> p n t"), func=ACT.Tanh, scale=0.5
            )

        def gain(eng, h, c0, c1):
            if h not in mb:
                t = work.tile([P, 512, 4], BF16, name="mb", tag="mb", bufs=3, align_bytes=64)
                mb[h] = t
            src = gmh
            eng.tensor_tensor(
                out=mb[h][:, c0:c1, :],
                in0=th[h][:, c0:c1, :],
                in1=src[:, h % 2, :].unsqueeze(1).to_broadcast([P, c1 - c0, 4]),
                op=ALU.mult,
            )

        mc, ms = {}, {}

        def quant_m(h, j=None):
            if h not in mc:
                a = work.tile([P, 512], U32, name="mc", tag="mc", bufs=10, align_bytes=64)
                b = work.tile([P, 512], U8, name="ms", tag="ms", bufs=10, align_bytes=64)
                mc[h], ms[h] = a, b
            cols = slice(0, 512) if j is None else slice(P * j, P * j + P)
            nc.vector.quantize_mx(
                out=mc[h][:, cols].bitcast(FP8X4),
                scales=ms[h][:, cols],
                in_=mb[h][:, cols, :].rearrange("p c t -> p (c t)"),
            )

        small = {}

        def col8(name):
            if name not in small:
                t = const.tile([P, 2, 4], F32, name=name, align_bytes=64)
                small[name] = t
            return small[name]

        zbank, ubank = {}, {}

        def class_logits(g):
            b = bank([P, 4, P], "O")
            for t in range(4):
                qs = slice(P * t, P * t + P)
                mx(b[:, t, :], codes["q", g][:, qs], scales["q", g][:, qs], wcls[:], wcls_sc[:], True, True)
            zbank[g] = b

        def void_logits():
            b = bank([P, 2, 4], "T")
            for g in range(2):
                for t in range(4):
                    for s in range(4):
                        nc.tensor.matmul(
                            b[:, g, t : t + 1],
                            lhsT=grouped["q", g][:, P * t : P * t + P, s],
                            rhs=wv[:, s : s + 1],
                            start=(s == 0),
                            stop=(s == 3),
                        )
            ubank[0] = b

        def softmax_max():
            u6, zm, nmx, ud = col8("u6"), col8("zm"), col8("nmx"), col8("ud")
            nc.vector.tensor_scalar(out=u6[:], in0=ubank[0][:], scalar1=6.0, scalar2=None, op0=ALU.add)
            for g in range(2):
                nc.vector.tensor_reduce(out=zm[:, g, :], in_=zbank[g][:], axis=AX.X, op=ALU.max)
            nc.vector.tensor_tensor(out=zm[:], in0=zm[:], in1=u6[:], op=ALU.max)
            nc.gpsimd.tensor_scalar(out=nmx[:], in0=zm[:], scalar1=-1.0, scalar2=None, op0=ALU.mult)
            nc.gpsimd.tensor_tensor(out=ud[:], in0=u6[:], in1=zm[:], op=ALU.subtract)

        ez = const.tile([P, 2, 4, P], F32, name="ez", align_bytes=64)
        sflat = const.tile([P, 2, 4, P], BF16, name="sflat", align_bytes=64)
        sb = const.tile([P, 2, P, 4], BF16, name="sb", align_bytes=64)
        s_cd = const.tile([P, 2, P], U32, name="s_cd", align_bytes=64)
        s_sc = const.tile([P, 2, P], U8, name="s_sc", align_bytes=64)

        def softmax_exp():
            rs, ev = col8("rs"), col8("ev")
            nmx, ud = col8("nmx"), col8("ud")
            nc.scalar.activation(out=ev[:], in_=ud[:], func=ACT.Exp)
            for g in range(2):
                for t in range(4):
                    nc.scalar.activation(
                        out=ez[:, g, t, :],
                        in_=zbank[g][:, t, :],
                        func=ACT.Exp,
                        bias=nmx[:, g, t : t + 1],
                        accum_out=rs[:, g, t : t + 1],
                    )

        def softmax_scores():
            rs, ev, den, rg, mean = col8("rs"), col8("ev"), col8("den"), col8("rg"), col8("mean")
            nc.gpsimd.tensor_tensor(out=den[:], in0=rs[:], in1=ev[:], op=ALU.add)
            nc.gpsimd.tensor_scalar(out=mean[:], in0=rs[:], scalar1=1.0 / C, scalar2=None, op0=ALU.mult)
            nc.vector.reciprocal(out=den[:], in_=den[:])
            nc.gpsimd.tensor_tensor(out=rg[:], in0=den[:], in1=gcf[:], op=ALU.mult)
            for g in range(2):
                for t in range(4):
                    nc.vector.tensor_scalar(
                        out=sflat[:, g, t, :],
                        in0=ez[:, g, t, :],
                        scalar1=mean[:, g, t : t + 1],
                        scalar2=rg[:, g, t : t + 1],
                        op0=ALU.subtract,
                        op1=ALU.mult,
                    )
                nc.vector.tensor_copy(out=sb[:, g, :, :], in_=sflat[:, g, :, :].rearrange("p t c -> p c t"))

        def quant_s():
            nc.vector.quantize_mx(
                out=s_cd[:].rearrange("p g c -> p (g c)").bitcast(FP8X4),
                scales=s_sc[:].rearrange("p g c -> p (g c)"),
                in_=sb[:].rearrange("p g c t -> p (g c t)"),
            )

        obank, pbank = {}, {}
        p_sc = const.tile([P, CHUNKS, P], U8, name="p_sc", align_bytes=64)
        pg, pcd = {}, {}

        def result_banks(c):
            obank[c] = bank([P, 512], "O")
            pbank[c] = bank([P, 4, P], "O")

        def product(c):
            for g in range(2):
                h = 2 * c + g
                mx(obank[c][:], s_cd[:, g, :], s_sc[:, g, :], mc[h][:], ms[h][:], g == 0, g == 1)
            for j in range(4):
                product_t(c, j)

        def product_t(c, j):
            px = slice(P * j, P * j + P)
            for g in range(2):
                h = 2 * c + g
                mx(pbank[c][:, j, :], mc[h][:, px], ms[h][:, px], s_cd[:, g, :], s_sc[:, g, :], g == 0, g == 1)

        def product_j(c, j):
            px = slice(P * j, P * j + P)
            for g in range(2):
                h = 2 * c + g
                mx(obank[c][:, px], s_cd[:, g, :], s_sc[:, g, :], mc[h][:, px], ms[h][:, px], g == 0, g == 1)
            product_t(c, j)

        def store_out(eng, c):
            t = work.tile([P, P, 4], F32, name="res", tag="res", bufs=2, align_bytes=64)
            copy(eng, t[:], obank[c][:].rearrange("p (j n) -> p n j", j=4))
            nc.sync.dma_start(out=out_0[:, 512 * c : 512 * c + 512], in_=t[:].rearrange("p n j -> p (n j)"))

        def fetch_p(eng, c):
            t = work.tile([P, P, 4], BF16, name="pg", tag="pg", bufs=2, align_bytes=64)
            copy(eng, t[:], pbank[c][:].rearrange("p j m -> p m j"))
            pg[c] = t

        def quant_p(c):
            t = work.tile([P, P], U32, name="pcd", tag="pcd", bufs=2, align_bytes=64)
            nc.vector.quantize_mx(
                out=t[:].bitcast(FP8X4), scales=p_sc[:, c, :], in_=pg[c][:].rearrange("p m j -> p (m j)")
            )
            nc.sync.dma_start(out=out_1[c].rearrange("p m t -> p (m t)").bitcast(I32), in_=t[:].bitcast(I32))

        def store_scales(c0, c1):
            for b in range(4):
                nc.sync.dma_start(
                    out=out_2[c0:c1, 4 * b : 4 * b + 4, :].rearrange("c r m -> r c m").bitcast(I32),
                    in_=p_sc[32 * b : 32 * b + 4, c0:c1, :].bitcast(I32),
                )

        def key(w):
            return (w[0], w[1])

        def run(eng, it):
            k = it[0]
            if k == "f": fetch(eng, it[1], it[2])
            elif k == "q": quant(it[1])
            elif k == "qh": quant(it[1], it[2])
            elif k == "o": store_out(eng, it[1])
            elif k == "P": fetch_p(eng, it[1])
            elif k == "qp": quant_p(it[1])
            elif k == "smax": softmax_max()
            elif k == "sexp": softmax_exp()
            elif k == "ssc": softmax_scores()
            elif k == "qs": quant_s()
            elif k == "gains":
                gains()

        for h in range(-1, TICKS + 1):
            for pos in range(5):
                if pos == 3 and 0 <= h < TICKS:
                    for it in PLAN["s"].get((h, 0), []):
                        run("S", it)
                    tanh(h, 0)
                for it in PLAN["pe"].get((h, pos), []):
                    if it[0] == "t":
                        turn(it[1], it[2], it[3])
                    elif it[0] == "z":
                        class_logits(0)
                        class_logits(1)
                        void_logits()
                    elif it[0] == "pr":
                        result_banks(it[1])
                        product(it[1])
                if pos < 4 and 0 <= h < TICKS:
                    logits(h, pos)
            if h == TICKS:
                c = CHUNKS - 1
                store_scales(0, c)
                result_banks(c)
                for j in range(4):
                    product_j(c, j)
                fetch_p("V", c)
                store_out("S", c)
                quant_p(c)
                store_scales(c, c + 1)
                continue
            if h == -1:
                for pos in range(12):
                    for it in PLAN["s"].get((h, pos), []):
                        run("S", it)
                    for it in PLAN["v"].get((h, pos), []):
                        run("V", it)
                continue
            for pos in range(1, 5):
                for it in PLAN["s"].get((h, pos), []):
                    run("S", it)
                if pos < 4:
                    tanh(h, pos)
            V = PLAN["v"]
            W = PLAN["W"] if h < TICKS - 1 else 0
            for c0 in range(0, W, PLAN["GP"]):
                gain(nc.gpsimd, h, c0, min(W, c0 + PLAN["GP"]))
            if h < TICKS - 1:
                for it in V.get((h, 0), []): run("V", it)
                gain(nc.vector, h, W, 256)
                if h > 0: quant_m(h - 1)
                for it in V.get((h, 1), []): run("V", it)
                gain(nc.vector, h, 256, 512)
                for it in V.get((h, 2), []): run("V", it)
            else:
                for it in V.get((h, 0), []): run("V", it)
                gain(nc.vector, h, 0, 128)
                quant_m(h - 1)
                for it in V.get((h, 1), []): run("V", it)
                gain(nc.vector, h, 128, 256)
                quant_m(h, 0)
                gain(nc.vector, h, 256, 384)
                quant_m(h, 1)
                gain(nc.vector, h, 384, 512)
                quant_m(h, 2)
                for it in V.get((h, 2), []): run("V", it)
                quant_m(h, 3)
